import numpy as np
import ml_dtypes


def mxq(x, axis, fmt="e4m3"):
    dtype, down = {"e4m3": (ml_dtypes.float8_e4m3fn, 7), "e5m2": (ml_dtypes.float8_e5m2, 14)}[fmt]
    v = np.moveaxis(np.asarray(x, np.float32).astype(ml_dtypes.bfloat16).astype(np.float64), axis, -1)
    blocks = v.reshape(v.shape[:-1] + (-1, 32))
    amax = np.abs(blocks).max(-1, keepdims=True)
    byte = np.maximum(np.where(amax > 0, np.frexp(amax)[1] - 1 + 127, 0) - down, 1)
    scale = np.exp2(byte - 127.0)
    codes = (blocks / scale).astype(np.float32).astype(dtype).astype(np.float64)
    return np.moveaxis((codes * scale).reshape(v.shape), -1, axis)


WIDE = False


def mx_kscale(k):
    if not WIDE:
        return np.ones(k)
    levels = np.array([10, -10, 5, -5, 0])
    if k % 512:
        return np.exp2(np.random.permutation(np.resize(levels, k // 32))).repeat(32)
    a = np.empty((k // 512, 16))
    for p in range(k // 512):
        a[p, :8] = np.random.permutation(np.resize(levels, 8))
        for g in range(8):
            far = levels[np.abs(levels - a[p, g]) >= 10]
            a[p, g + 8] = far[np.random.randint(len(far))]
    return np.exp2(a.ravel()).repeat(32)


def f64(x):
    return np.asarray(x).astype(np.float64)


def striped(idx):
    return np.tile(idx.reshape(-1, 16).T, (8, 1)).astype(np.uint16)


def unstriped(offs):
    return offs[:16].T.reshape(-1).astype(np.int64)


def pack_weight(w):
    k, n = w.shape
    w = f64(np.asarray(w, np.float32).astype(ml_dtypes.bfloat16)).reshape(k // 32, 32, n)
    amax = np.abs(w).max(1)
    byte = np.clip(np.where(amax > 0, np.frexp(amax)[1] - 1 + 127 - 7, 1), 1, 254)
    scaled = (w * np.exp2(127.0 - byte)[:, None, :]).reshape(k, n).astype(np.float32)
    words = np.ascontiguousarray(scaled.reshape(k // 512, 128, 4, n).transpose(0, 1, 3, 2)).astype(ml_dtypes.float8_e4m3fn).view(np.uint8)
    return words, np.ascontiguousarray(byte.astype(np.uint8).reshape(k // 512, 16, n))


def unpack_weight(words, scales):
    g, p, n, _ = words.shape
    vals = np.ascontiguousarray(words).view(ml_dtypes.float8_e4m3fn).astype(np.float64) * np.repeat(np.exp2(scales.astype(np.float64) - 127.0), 8, axis=1)[..., None]
    return vals.transpose(0, 1, 3, 2).reshape(g * 512, n)


K, T, S, N = 1024, 2048, 1024, 256
P = 2 ** 7


def setup_inputs():
    n = np.random.standard_normal
    s = mx_kscale(K)[:, None]
    packed_w1 = pack_weight(n((K, N)) / np.sqrt(K) / s)
    return {
        "xT": (n((K, T)) * s).astype(np.float32),
        "mean": np.tile(0.3 * np.random.standard_normal(T), (P, 1)).astype(np.float32),
        "inv": np.tile(np.random.uniform(0.5, 2.0, T), (P, 1)).astype(np.float32),
        "gsum": n((N, 1)).astype(np.float32),
        "b": (0.3 * n((N, 1))).astype(np.float32),
        "w1_words": packed_w1[0],
        "w1_scales": packed_w1[1],
        "offs": striped(np.random.permutation(T)[:S]),
    }


def reference(xT, mean, inv, gsum, b, w1_words, w1_scales, offs):
    xq = mxq(f64(xT)[:, unstriped(offs)], 0, "e4m3")
    y = unpack_weight(w1_words, w1_scales).T @ xq
    mg = f64(mean)[:1][:, unstriped(offs)]
    ig = f64(inv)[:1][:, unstriped(offs)]
    return (y - (f64(gsum) * mg)) * ig + f64(b)

@@ -1,0 +1,216 @@
+from contextlib import ExitStack
+
+import concourse.mybir as mybir
+from concourse.masks import make_identity
+
+K, T, S, N = 1024, 2048, 1024, 256
+FLOPS = 2 * K * S * N
+BYTES = 4 * (K * T + 2 * T + 2 * N + N * S) + K * N + K * N // 32 + 2 * 128 * (S // 16)
+
+F32 = mybir.dt.float32
+BF16 = mybir.dt.bfloat16
+I32 = mybir.dt.int32
+U32 = mybir.dt.uint32
+U16 = mybir.dt.uint16
+U8 = mybir.dt.uint8
+FP8X4 = mybir.dt.float8_e4m3fn_x4
+MULT = mybir.AluOpType.mult
+ADD = mybir.AluOpType.add
+IDENTITY = mybir.ActivationFunctionType.Identity
+
+P = 128
+PASSES = K // 512
+SLICE = 256
+SLICES = S // SLICE
+BLOCKS = S // P
+EARLY_BLOCKS = 6
+PAIR_CHUNKS = (
+    ((0, 1024, 1024), (1024, 2048, 1024)),
+    ((0, 1024, 1024), (1024, 2048, 352)),
+    ((0, 1024, 1024), (1024, 2048, 768)),
+    ((0, 1024, 1024), (1024, 1536, 0), (1536, 1792, 256), (1792, 2048, 0)),
+)
+PIECE = (512, 256)
+GATHER = (1024, 512, 1024, 256)
+
+
+def tile_picked_lnfold_none_l_kernel(
+    tc, xT, mean, inv, gsum, b, w1_words, w1_scales, offs, out
+):
+    nc = tc.nc
+    with ExitStack() as ctx:
+        keep = ctx.enter_context(tc.tile_pool(name="keep", bufs=1))
+        psum = ctx.enter_context(tc.psum_pool(name="psum", bufs=1))
+
+        offsets = keep.tile([P, S // 16], U16, name="offsets")
+        x_rows = xT.rearrange("(g p u e) t -> g u p e t", g=PASSES, p=P, u=2, e=2)
+        pair_chunks = PAIR_CHUNKS
+
+        stats = keep.tile([P, T], F32, name="stats")
+        nc.vector.memset(stats[:], 0.0)
+        stat_rows = keep.tile([2, T], F32, name="stat_rows")
+        nc.sync.dma_start(out=stat_rows[0:1, :], in_=mean[0:1, :])
+        nc.sync.dma_start(out=stat_rows[1:2, :], in_=inv[0:1, :])
+        nc.sync.dma_start(offsets[:], offs)
+        nc.vector.tensor_copy(stats[0:2, :], stat_rows[:])
+        g_col = keep.tile([P, 2], F32, name="g_col")
+        b_col = keep.tile([P, 2], F32, name="b_col")
+        w_scales = keep.tile([P, N], U8, name="w_scales", align_bytes=64)
+        nc.gpsimd.memset(w_scales[:].bitcast(I32), 0)
+        ident = keep.tile([P, P], F32, name="ident")
+        make_identity(nc, ident[:])
+        with nc.allow_non_contiguous_dma(reason="one value a partition"):
+            nc.scalar.dma_start(out=g_col[:], in_=gsum.rearrange("(c p) o -> p (c o)", p=P))
+        raw = {}
+        for q in range(4):
+            for c, (t0, t1, ts) in enumerate(pair_chunks[q]):
+                raw[q, c] = keep.tile([P, 2, t1 - t0], F32, name="raw%d_%d" % (q, c))
+                nc.sync.dma_start(out=raw[q, c][:], in_=x_rows[q // 2, q % 2, :, :, t0:t1])
+                if q > 0 and c == 0:
+                    for quad in ((0, 1), (2, 3), ())[q - 1]:
+                        nc.sync.dma_start(
+                            out=w_scales[32 * quad : 32 * quad + 4 * PASSES, :].bitcast(I32),
+                            in_=w1_scales[:, 4 * quad : 4 * quad + 4, :].bitcast(I32),
+                        )
+                if q == 3 and c == 0:
+                    with nc.allow_non_contiguous_dma(reason="one value a partition"):
+                        nc.sync.dma_start(out=b_col[:], in_=b.rearrange("(c p) o -> p (c o)", p=P))
+        w_codes = keep.tile([P, PASSES, N], U32, name="w_codes", align_bytes=64)
+        nc.sync.dma_start(
+            out=w_codes[:].bitcast(I32),
+            in_=w1_words.rearrange("g p n t -> p g (n t)").bitcast(I32),
+        )
+
+        picked_stats = keep.tile([P, S], F32, name="picked_stats")
+        nc.vector.tensor_copy(picked_stats[:], stats[:].indirect(offsets[:]))
+        stat_cols = keep.tile([P, BLOCKS, 2], F32, name="stat_cols")
+        for h in range(2):
+            turned = psum.tile([P, 4, P], F32, name="turned%d" % h, tag="bank%d" % (6 + h))
+            for i in range(4):
+                j = 4 * h + i
+                nc.tensor.transpose(turned[:, i, :], picked_stats[:, j * P : (j + 1) * P], ident[:])
+            nc.vector.tensor_copy(stat_cols[:, 4 * h : 4 * h + 4, :], turned[:, :, 0:2])
+        g_spread = psum.tile([P, 2, P], F32, name="g_spread", tag="bank5")
+        for c in range(2):
+            nc.tensor.transpose(g_spread[:, c, :], g_col[:, c : c + 1].to_broadcast([P, P]), ident[:])
+        neg_g = keep.tile([P, N], F32, name="neg_g")
+        nc.vector.tensor_scalar(neg_g[:], g_spread[:].rearrange("p c m -> p (c m)"), -1.0, None, MULT)
+        shift = keep.tile([P, BLOCKS, N], F32, name="shift")
+        for j in range(BLOCKS):
+            nc.vector.tensor_scalar(
+                shift[:, j, :], neg_g[:], stat_cols[:, j, 0:1], stat_cols[:, j, 1:2], MULT, MULT
+            )
+
+        pairs = [keep.tile([P, 2 * T], BF16, name="pairs%d" % q, align_bytes=64) for q in range(4)]
+        picked = {}
+        codes = {}
+        scales = {}
+        for g in range(PASSES):
+            picked[g] = keep.tile([P, 2, S], U32, name="picked%d" % g, align_bytes=64)
+
+        def cast(q):
+            for c, (t0, t1, ts) in enumerate(pair_chunks[q]):
+                src = raw[q, c][:].rearrange("p e t -> p t e")
+                dst = pairs[q][:, 2 * t0 : 2 * t1].rearrange("p (t e) -> p t e", e=2)
+                if ts > 0:
+                    nc.scalar.activation(dst[:, 0:ts, :], src[:, 0:ts, :], IDENTITY)
+                if ts < t1 - t0:
+                    nc.vector.tensor_copy(dst[:, ts:, :], src[:, ts:, :])
+
+        def gather(q, s):
+            n = GATHER[q]
+            cols = offsets[:, s * (n // 16) : (s + 1) * (n // 16)]
+            nc.vector.tensor_copy(
+                picked[q // 2][:, q % 2, s * n : (s + 1) * n], pairs[q][:].bitcast(U32).indirect(cols)
+            )
+
+        woven = {}
+
+        def weave(g, s, on_scalar):
+            n = PIECE[g]
+            woven[g, s] = keep.tile([P, 4 * n], BF16, name="woven%d_%d" % (g, s), align_bytes=64)
+            src = picked[g][:, :, s * n : (s + 1) * n]
+            if on_scalar:
+                nc.scalar.copy(
+                    woven[g, s][:].bitcast(U32).rearrange("p (n u) -> p n u", u=2), src.rearrange("p u n -> p n u")
+                )
+            else:
+                nc.vector.tensor_copy(
+                    woven[g, s][:].bitcast(I32).rearrange("p (n u) -> p n u", u=2),
+                    src.bitcast(I32).rearrange("p u n -> p n u"),
+                )
+
+        def quantize(g, s):
+            n = PIECE[g]
+            codes[g, s] = keep.tile([P, n], U32, name="codes%d_%d" % (g, s), align_bytes=64)
+            scales[g, s] = keep.tile([P, n], U8, name="scales%d_%d" % (g, s), align_bytes=64)
+            nc.vector.quantize_mx(out=codes[g, s][:].bitcast(FP8X4), scales=scales[g, s][:], in_=woven[g, s][:])
+
+        sums = {}
+
+        def multiply(g, j):
+            if g == 0:
+                sums[j] = psum.tile([P, N], F32, name="sums%d" % j, tag="bank%d" % (j % EARLY_BLOCKS))
+            s, i = divmod(j, PIECE[g] // P)
+            cols = slice(i * P, (i + 1) * P)
+            nc.tensor.matmul_mx(
+                out=sums[j][:],
+                lhsT=codes[g, s][:, cols].bitcast(FP8X4),
+                lhsT_scale=scales[g, s][:, cols],
+                rhs=w_codes[:, g, :].bitcast(FP8X4),
+                rhs_scale=w_scales[4 * g : P, :],
+                start=(g == 0),
+                stop=(g == PASSES - 1),
+            )
+
+        scaled = {}
+
+        def correct(j):
+            scaled[j] = keep.tile([P, N], F32, name="scaled%d" % j)
+            nc.vector.scalar_tensor_tensor(
+                scaled[j][:], sums[j][:], stat_cols[:, j, 1:2], shift[:, j, :], MULT, ADD
+            )
+
+        out_rows = out.rearrange("(c p) s -> p c s", p=P)
+
+        def finish(s):
+            back = psum.tile([P, 2, SLICE], F32, name="back%d" % s, tag="bank%d" % (6 + s % 2))
+            for i in range(2):
+                for c in range(2):
+                    nc.tensor.transpose(
+                        back[:, c, i * P : (i + 1) * P], scaled[2 * s + i][:, c * P : (c + 1) * P], ident[:]
+                    )
+            result = keep.tile([P, 2, SLICE], F32, name="result%d" % s)
+            for c in range(2):
+                nc.scalar.activation(result[:, c, :], back[:, c, :], IDENTITY, bias=b_col[:, c : c + 1])
+            nc.sync.dma_start(out=out_rows[:, :, s * SLICE : (s + 1) * SLICE], in_=result[:])
+
+        for q in range(2):
+            cast(q)
+            for s in range(S // GATHER[q]):
+                gather(q, s)
+        for s in range(2):
+            weave(0, s, False)
+        for s in range(2):
+            quantize(0, s)
+        cast(2)
+        gather(2, 0)
+        cast(3)
+        for j in range(EARLY_BLOCKS):
+            multiply(0, j)
+        for step in range(SLICES + 3):
+            if step < SLICES:
+                gather(3, step)
+                weave(1, step, True)
+            s = step - 1
+            if 0 <= s < SLICES:
+                quantize(1, s)
+                for j in (2 * s, 2 * s + 1):
+                    if j >= EARLY_BLOCKS:
+                        multiply(0, j)
+                    multiply(1, j)
+            s = step - 2
+            if 0 <= s < SLICES:
+                correct(2 * s)
+                correct(2 * s + 1)
+                finish(s)

@@ -23,12 +23,12 @@ PASSES = K // 512
 SLICE = 256
 SLICES = S // SLICE
 BLOCKS = S // P
-EARLY_BLOCKS = 6
+SCALAR_BLOCKS = 4
 PAIR_CHUNKS = (
-    ((0, 1024, 1024), (1024, 2048, 1024)),
-    ((0, 1024, 1024), (1024, 2048, 352)),
-    ((0, 1024, 1024), (1024, 2048, 768)),
-    ((0, 1024, 1024), (1024, 1536, 0), (1536, 1792, 256), (1792, 2048, 0)),
+    ((0, 256, 256), (256, 1024, 768), (1024, 2048, 1024)),
+    ((0, 1024, 1024), (1024, 2048, 688)),
+    ((0, 1024, 1024), (1024, 2048, 832)),
+    ((0, 1024, 1024), (1024, 1536, 0), (1536, 1792, 256), (1792, 2048, 80)),
 )
 PIECE = (512, 256)
 GATHER = (1024, 512, 1024, 256)
@@ -46,43 +46,51 @@ def tile_picked_lnfold_none_l_kernel(
         x_rows = xT.rearrange("(g p u e) t -> g u p e t", g=PASSES, p=P, u=2, e=2)
         pair_chunks = PAIR_CHUNKS
 
-        stats = keep.tile([P, T], F32, name="stats")
-        nc.vector.memset(stats[:], 0.0)
+        stats = keep.tile([P, T + N], F32, name="stats")
+        nc.vector.memset(stats[:, 0 : T // 2], 0.0)
+        nc.gpsimd.memset(stats[:, T // 2 : T + N], 0.0)
         stat_rows = keep.tile([2, T], F32, name="stat_rows")
+        chan_rows = keep.tile([2, N], F32, name="chan_rows")
         nc.sync.dma_start(out=stat_rows[0:1, :], in_=mean[0:1, :])
-        nc.sync.dma_start(out=stat_rows[1:2, :], in_=inv[0:1, :])
         nc.sync.dma_start(offsets[:], offs)
-        nc.vector.tensor_copy(stats[0:2, :], stat_rows[:])
-        g_col = keep.tile([P, 2], F32, name="g_col")
-        b_col = keep.tile([P, 2], F32, name="b_col")
+        nc.scalar.dma_start(out=chan_rows[0:1, :], in_=gsum.rearrange("n o -> o n"))
+        nc.scalar.dma_start(out=chan_rows[1:2, :], in_=b.rearrange("n o -> o n"))
+        nc.scalar.dma_start(out=stat_rows[1:2, :], in_=inv[0:1, :])
+        nc.vector.tensor_copy(stats[0:2, T : T + N], chan_rows[:])
+        nc.vector.tensor_copy(stats[0:2, 0:T], stat_rows[:])
         w_scales = keep.tile([P, N], U8, name="w_scales", align_bytes=64)
         nc.gpsimd.memset(w_scales[:].bitcast(I32), 0)
         ident = keep.tile([P, P], F32, name="ident")
         make_identity(nc, ident[:])
-        with nc.allow_non_contiguous_dma(reason="one value a partition"):
-            nc.scalar.dma_start(out=g_col[:], in_=gsum.rearrange("(c p) o -> p (c o)", p=P))
         raw = {}
         for q in range(4):
             for c, (t0, t1, ts) in enumerate(pair_chunks[q]):
-                raw[q, c] = keep.tile([P, 2, t1 - t0], F32, name="raw%d_%d" % (q, c))
+                raw[q, c] = keep.tile(
+                    [P, 2, t1 - t0], F32, name="raw%d_%d" % (q, c), tag="raw%d_%d" % (q, c), align_bytes=64
+                )
                 nc.sync.dma_start(out=raw[q, c][:], in_=x_rows[q // 2, q % 2, :, :, t0:t1])
-                if q > 0 and c == 0:
-                    for quad in ((0, 1), (2, 3), ())[q - 1]:
-                        nc.sync.dma_start(
-                            out=w_scales[32 * quad : 32 * quad + 4 * PASSES, :].bitcast(I32),
-                            in_=w1_scales[:, 4 * quad : 4 * quad + 4, :].bitcast(I32),
-                        )
-                if q == 3 and c == 0:
-                    with nc.allow_non_contiguous_dma(reason="one value a partition"):
-                        nc.sync.dma_start(out=b_col[:], in_=b.rearrange("(c p) o -> p (c o)", p=P))
-        w_codes = keep.tile([P, PASSES, N], U32, name="w_codes", align_bytes=64)
-        nc.sync.dma_start(
-            out=w_codes[:].bitcast(I32),
-            in_=w1_words.rearrange("g p n t -> p g (n t)").bitcast(I32),
-        )
+        for quad in range(4):
+            nc.sync.dma_start(
+                out=w_scales[32 * quad : 32 * quad + 4 * PASSES, :].bitcast(I32),
+                in_=w1_scales[:, 4 * quad : 4 * quad + 4, :].bitcast(I32),
+            )
 
+        chan_turned = psum.tile([P, 2, P], F32, name="chan_turned", tag="bank4")
+        for c in range(2):
+            nc.tensor.transpose(chan_turned[:, c, :], stats[:, T + c * P : T + (c + 1) * P], ident[:])
+        chan_cols = keep.tile([P, 2, 2], F32, name="chan_cols")
+        nc.vector.tensor_copy(chan_cols[:], chan_turned[:, :, 0:2])
+        g_spread = psum.tile([P, 2, P], F32, name="g_spread", tag="bank5")
+        for c in range(2):
+            nc.tensor.transpose(g_spread[:, c, :], chan_cols[:, c, 0:1].to_broadcast([P, P]), ident[:])
+        neg_g = keep.tile([P, N], F32, name="neg_g")
+        nc.vector.tensor_scalar(neg_g[:], g_spread[:].rearrange("p c m -> p (c m)"), -1.0, None, MULT)
         picked_stats = keep.tile([P, S], F32, name="picked_stats")
-        nc.vector.tensor_copy(picked_stats[:], stats[:].indirect(offsets[:]))
+        for h in range(2):
+            nc.vector.tensor_copy(
+                picked_stats[:, h * (S // 2) : (h + 1) * (S // 2)],
+                stats[:, 0:T].indirect(offsets[:, h * (S // 32) : (h + 1) * (S // 32)]),
+            )
         stat_cols = keep.tile([P, BLOCKS, 2], F32, name="stat_cols")
         for h in range(2):
             turned = psum.tile([P, 4, P], F32, name="turned%d" % h, tag="bank%d" % (6 + h))
@@ -90,11 +98,6 @@ def tile_picked_lnfold_none_l_kernel(
                 j = 4 * h + i
                 nc.tensor.transpose(turned[:, i, :], picked_stats[:, j * P : (j + 1) * P], ident[:])
             nc.vector.tensor_copy(stat_cols[:, 4 * h : 4 * h + 4, :], turned[:, :, 0:2])
-        g_spread = psum.tile([P, 2, P], F32, name="g_spread", tag="bank5")
-        for c in range(2):
-            nc.tensor.transpose(g_spread[:, c, :], g_col[:, c : c + 1].to_broadcast([P, P]), ident[:])
-        neg_g = keep.tile([P, N], F32, name="neg_g")
-        nc.vector.tensor_scalar(neg_g[:], g_spread[:].rearrange("p c m -> p (c m)"), -1.0, None, MULT)
         shift = keep.tile([P, BLOCKS, N], F32, name="shift")
         for j in range(BLOCKS):
             nc.vector.tensor_scalar(
@@ -150,7 +153,7 @@ def tile_picked_lnfold_none_l_kernel(
 
         def multiply(g, j):
             if g == 0:
-                sums[j] = psum.tile([P, N], F32, name="sums%d" % j, tag="bank%d" % (j % EARLY_BLOCKS))
+                sums[j] = psum.tile([P, N], F32, name="sums%d" % j, tag="bank%d" % j)
             s, i = divmod(j, PIECE[g] // P)
             cols = slice(i * P, (i + 1) * P)
             nc.tensor.matmul_mx(
@@ -167,23 +170,31 @@ def tile_picked_lnfold_none_l_kernel(
 
         def correct(j):
             scaled[j] = keep.tile([P, N], F32, name="scaled%d" % j)
-            nc.vector.scalar_tensor_tensor(
-                scaled[j][:], sums[j][:], stat_cols[:, j, 1:2], shift[:, j, :], MULT, ADD
-            )
+            if j < SCALAR_BLOCKS:
+                nc.scalar.activation(scaled[j][:], sums[j][:], IDENTITY, scale=stat_cols[:, j, 1:2])
+            else:
+                nc.vector.scalar_tensor_tensor(
+                    scaled[j][:], sums[j][:], stat_cols[:, j, 1:2], shift[:, j, :], MULT, ADD
+                )
 
-        out_rows = out.rearrange("(c p) s -> p c s", p=P)
-
-        def finish(s):
-            back = psum.tile([P, 2, SLICE], F32, name="back%d" % s, tag="bank%d" % (6 + s % 2))
-            for i in range(2):
-                for c in range(2):
-                    nc.tensor.transpose(
-                        back[:, c, i * P : (i + 1) * P], scaled[2 * s + i][:, c * P : (c + 1) * P], ident[:]
-                    )
-            result = keep.tile([P, 2, SLICE], F32, name="result%d" % s)
+        def finish(blocks, first_bank, share):
+            width = len(blocks) * P
             for c in range(2):
-                nc.scalar.activation(result[:, c, :], back[:, c, :], IDENTITY, bias=b_col[:, c : c + 1])
-            nc.sync.dma_start(out=out_rows[:, :, s * SLICE : (s + 1) * SLICE], in_=result[:])
+                rows = slice(c * P, (c + 1) * P)
+                back = psum.tile([P, width], F32, name="back%d_%d" % (blocks[0], c), tag="bank%d" % (first_bank + c))
+                for i, j in enumerate(blocks):
+                    dst = back[:, i * P : (i + 1) * P]
+                    if j < SCALAR_BLOCKS:
+                        nc.tensor.matmul(dst, shift[:, j, rows], ident[:], start=True, stop=False, is_transpose=True)
+                        nc.tensor.matmul(dst, scaled[j][:, rows], ident[:], start=False, stop=True, is_transpose=True)
+                    else:
+                        nc.tensor.transpose(dst, scaled[j][:, rows], ident[:])
+                result = keep.tile([P, width], F32, name="result%d_%d" % (blocks[0], c))
+                if share and c == 1:
+                    nc.vector.tensor_scalar(result[:], back[:], chan_cols[:, c, 1:2], None, ADD)
+                else:
+                    nc.scalar.activation(result[:], back[:], IDENTITY, bias=chan_cols[:, c, 1:2])
+                nc.sync.dma_start(out=out[rows, blocks[0] * P : blocks[0] * P + width], in_=result[:])
 
         for q in range(2):
             cast(q)
@@ -196,21 +207,24 @@ def tile_picked_lnfold_none_l_kernel(
         cast(2)
         gather(2, 0)
         cast(3)
-        for j in range(EARLY_BLOCKS):
+        w_codes = keep.tile([P, PASSES, N], U32, name="w_codes", tag="raw3_0", align_bytes=64)
+        nc.sync.dma_start(
+            out=w_codes[:].bitcast(I32),
+            in_=w1_words.rearrange("g p n t -> p g (n t)").bitcast(I32),
+        )
+        for j in range(BLOCKS):
             multiply(0, j)
-        for step in range(SLICES + 3):
-            if step < SLICES:
-                gather(3, step)
-                weave(1, step, True)
-            s = step - 1
-            if 0 <= s < SLICES:
-                quantize(1, s)
-                for j in (2 * s, 2 * s + 1):
-                    if j >= EARLY_BLOCKS:
-                        multiply(0, j)
-                    multiply(1, j)
-            s = step - 2
-            if 0 <= s < SLICES:
-                correct(2 * s)
-                correct(2 * s + 1)
-                finish(s)
+        for s in range(SLICES):
+            gather(3, s)
+            weave(1, s, True)
+        for s in range(SLICES):
+            quantize(1, s)
+            multiply(1, 2 * s)
+            multiply(1, 2 * s + 1)
+        for s in range(SLICES - 1):
+            correct(2 * s)
+            correct(2 * s + 1)
+            finish((2 * s, 2 * s + 1), 2 * s, s == SLICES - 2)
+        for i in range(2):
+            correct(BLOCKS - 2 + i)
+            finish((BLOCKS - 2 + i,), 2 * i, True)

from contextlib import ExitStack

import concourse.mybir as mybir
from concourse.masks import make_identity

K, T, S, N = 1024, 2048, 1024, 256
FLOPS = 2 * K * S * N
BYTES = 4 * (K * T + 2 * T + 2 * N + N * S) + K * N + K * N // 32 + 2 * 128 * (S // 16)

F32 = mybir.dt.float32
BF16 = mybir.dt.bfloat16
I32 = mybir.dt.int32
U32 = mybir.dt.uint32
U16 = mybir.dt.uint16
U8 = mybir.dt.uint8
FP8X4 = mybir.dt.float8_e4m3fn_x4
MULT = mybir.AluOpType.mult
ADD = mybir.AluOpType.add
IDENTITY = mybir.ActivationFunctionType.Identity

P = 128
PASSES = K // 512
SLICE = 256
SLICES = S // SLICE
BLOCKS = S // P
SCALAR_BLOCKS = 4
PAIR_CHUNKS = (
    ((0, 256, 256), (256, 1024, 768), (1024, 2048, 1024)),
    ((0, 1024, 1024), (1024, 2048, 688)),
    ((0, 1024, 1024), (1024, 2048, 832)),
    ((0, 1024, 1024), (1024, 1536, 0), (1536, 1792, 256), (1792, 2048, 80)),
)
PIECE = (512, 256)
GATHER = (1024, 512, 1024, 256)


def tile_picked_lnfold_none_l_kernel(
    tc, xT, mean, inv, gsum, b, w1_words, w1_scales, offs, out
):
    nc = tc.nc
    with ExitStack() as ctx:
        keep = ctx.enter_context(tc.tile_pool(name="keep", bufs=1))
        psum = ctx.enter_context(tc.psum_pool(name="psum", bufs=1))

        offsets = keep.tile([P, S // 16], U16, name="offsets")
        x_rows = xT.rearrange("(g p u e) t -> g u p e t", g=PASSES, p=P, u=2, e=2)
        pair_chunks = PAIR_CHUNKS

        stats = keep.tile([P, T + N], F32, name="stats")
        nc.vector.memset(stats[:, 0 : T // 2], 0.0)
        nc.gpsimd.memset(stats[:, T // 2 : T + N], 0.0)
        stat_rows = keep.tile([2, T], F32, name="stat_rows")
        chan_rows = keep.tile([2, N], F32, name="chan_rows")
        nc.sync.dma_start(out=stat_rows[0:1, :], in_=mean[0:1, :])
        nc.sync.dma_start(offsets[:], offs)
        nc.scalar.dma_start(out=chan_rows[0:1, :], in_=gsum.rearrange("n o -> o n"))
        nc.scalar.dma_start(out=chan_rows[1:2, :], in_=b.rearrange("n o -> o n"))
        nc.scalar.dma_start(out=stat_rows[1:2, :], in_=inv[0:1, :])
        nc.vector.tensor_copy(stats[0:2, T : T + N], chan_rows[:])
        nc.vector.tensor_copy(stats[0:2, 0:T], stat_rows[:])
        w_scales = keep.tile([P, N], U8, name="w_scales", align_bytes=64)
        nc.gpsimd.memset(w_scales[:].bitcast(I32), 0)
        ident = keep.tile([P, P], F32, name="ident")
        make_identity(nc, ident[:])
        raw = {}
        for q in range(4):
            for c, (t0, t1, ts) in enumerate(pair_chunks[q]):
                raw[q, c] = keep.tile(
                    [P, 2, t1 - t0], F32, name="raw%d_%d" % (q, c), tag="raw%d_%d" % (q, c), align_bytes=64
                )
                nc.sync.dma_start(out=raw[q, c][:], in_=x_rows[q // 2, q % 2, :, :, t0:t1])
        for quad in range(4):
            nc.sync.dma_start(
                out=w_scales[32 * quad : 32 * quad + 4 * PASSES, :].bitcast(I32),
                in_=w1_scales[:, 4 * quad : 4 * quad + 4, :].bitcast(I32),
            )

        chan_turned = psum.tile([P, 2, P], F32, name="chan_turned", tag="bank4")
        for c in range(2):
            nc.tensor.transpose(chan_turned[:, c, :], stats[:, T + c * P : T + (c + 1) * P], ident[:])
        chan_cols = keep.tile([P, 2, 2], F32, name="chan_cols")
        nc.vector.tensor_copy(chan_cols[:], chan_turned[:, :, 0:2])
        g_spread = psum.tile([P, 2, P], F32, name="g_spread", tag="bank5")
        for c in range(2):
            nc.tensor.transpose(g_spread[:, c, :], chan_cols[:, c, 0:1].to_broadcast([P, P]), ident[:])
        neg_g = keep.tile([P, N], F32, name="neg_g")
        nc.vector.tensor_scalar(neg_g[:], g_spread[:].rearrange("p c m -> p (c m)"), -1.0, None, MULT)
        picked_stats = keep.tile([P, S], F32, name="picked_stats")
        for h in range(2):
            nc.vector.tensor_copy(
                picked_stats[:, h * (S // 2) : (h + 1) * (S // 2)],
                stats[:, 0:T].indirect(offsets[:, h * (S // 32) : (h + 1) * (S // 32)]),
            )
        stat_cols = keep.tile([P, BLOCKS, 2], F32, name="stat_cols")
        for h in range(2):
            turned = psum.tile([P, 4, P], F32, name="turned%d" % h, tag="bank%d" % (6 + h))
            for i in range(4):
                j = 4 * h + i
                nc.tensor.transpose(turned[:, i, :], picked_stats[:, j * P : (j + 1) * P], ident[:])
            nc.vector.tensor_copy(stat_cols[:, 4 * h : 4 * h + 4, :], turned[:, :, 0:2])
        shift = keep.tile([P, BLOCKS, N], F32, name="shift")
        for j in range(BLOCKS):
            nc.vector.tensor_scalar(
                shift[:, j, :], neg_g[:], stat_cols[:, j, 0:1], stat_cols[:, j, 1:2], MULT, MULT
            )

        pairs = [keep.tile([P, 2 * T], BF16, name="pairs%d" % q, align_bytes=64) for q in range(4)]
        picked = {}
        codes = {}
        scales = {}
        for g in range(PASSES):
            picked[g] = keep.tile([P, 2, S], U32, name="picked%d" % g, align_bytes=64)

        def cast(q):
            for c, (t0, t1, ts) in enumerate(pair_chunks[q]):
                src = raw[q, c][:].rearrange("p e t -> p t e")
                dst = pairs[q][:, 2 * t0 : 2 * t1].rearrange("p (t e) -> p t e", e=2)
                if ts > 0:
                    nc.scalar.activation(dst[:, 0:ts, :], src[:, 0:ts, :], IDENTITY)
                if ts < t1 - t0:
                    nc.vector.tensor_copy(dst[:, ts:, :], src[:, ts:, :])

        def gather(q, s):
            n = GATHER[q]
            cols = offsets[:, s * (n // 16) : (s + 1) * (n // 16)]
            nc.vector.tensor_copy(
                picked[q // 2][:, q % 2, s * n : (s + 1) * n], pairs[q][:].bitcast(U32).indirect(cols)
            )

        woven = {}

        def weave(g, s, on_scalar):
            n = PIECE[g]
            woven[g, s] = keep.tile([P, 4 * n], BF16, name="woven%d_%d" % (g, s), align_bytes=64)
            src = picked[g][:, :, s * n : (s + 1) * n]
            if on_scalar:
                nc.scalar.copy(
                    woven[g, s][:].bitcast(U32).rearrange("p (n u) -> p n u", u=2), src.rearrange("p u n -> p n u")
                )
            else:
                nc.vector.tensor_copy(
                    woven[g, s][:].bitcast(I32).rearrange("p (n u) -> p n u", u=2),
                    src.bitcast(I32).rearrange("p u n -> p n u"),
                )

        def quantize(g, s):
            n = PIECE[g]
            codes[g, s] = keep.tile([P, n], U32, name="codes%d_%d" % (g, s), align_bytes=64)
            scales[g, s] = keep.tile([P, n], U8, name="scales%d_%d" % (g, s), align_bytes=64)
            nc.vector.quantize_mx(out=codes[g, s][:].bitcast(FP8X4), scales=scales[g, s][:], in_=woven[g, s][:])

        sums = {}

        def multiply(g, j):
            if g == 0:
                sums[j] = psum.tile([P, N], F32, name="sums%d" % j, tag="bank%d" % j)
            s, i = divmod(j, PIECE[g] // P)
            cols = slice(i * P, (i + 1) * P)
            nc.tensor.matmul_mx(
                out=sums[j][:],
                lhsT=codes[g, s][:, cols].bitcast(FP8X4),
                lhsT_scale=scales[g, s][:, cols],
                rhs=w_codes[:, g, :].bitcast(FP8X4),
                rhs_scale=w_scales[4 * g : P, :],
                start=(g == 0),
                stop=(g == PASSES - 1),
            )

        scaled = {}

        def correct(j):
            scaled[j] = keep.tile([P, N], F32, name="scaled%d" % j)
            if j < SCALAR_BLOCKS:
                nc.scalar.activation(scaled[j][:], sums[j][:], IDENTITY, scale=stat_cols[:, j, 1:2])
            else:
                nc.vector.scalar_tensor_tensor(
                    scaled[j][:], sums[j][:], stat_cols[:, j, 1:2], shift[:, j, :], MULT, ADD
                )

        def finish(blocks, first_bank, share):
            width = len(blocks) * P
            for c in range(2):
                rows = slice(c * P, (c + 1) * P)
                back = psum.tile([P, width], F32, name="back%d_%d" % (blocks[0], c), tag="bank%d" % (first_bank + c))
                for i, j in enumerate(blocks):
                    dst = back[:, i * P : (i + 1) * P]
                    if j < SCALAR_BLOCKS:
                        nc.tensor.matmul(dst, shift[:, j, rows], ident[:], start=True, stop=False, is_transpose=True)
                        nc.tensor.matmul(dst, scaled[j][:, rows], ident[:], start=False, stop=True, is_transpose=True)
                    else:
                        nc.tensor.transpose(dst, scaled[j][:, rows], ident[:])
                result = keep.tile([P, width], F32, name="result%d_%d" % (blocks[0], c))
                if share and c == 1:
                    nc.vector.tensor_scalar(result[:], back[:], chan_cols[:, c, 1:2], None, ADD)
                else:
                    nc.scalar.activation(result[:], back[:], IDENTITY, bias=chan_cols[:, c, 1:2])
                nc.sync.dma_start(out=out[rows, blocks[0] * P : blocks[0] * P + width], in_=result[:])

        for q in range(2):
            cast(q)
            for s in range(S // GATHER[q]):
                gather(q, s)
        for s in range(2):
            weave(0, s, False)
        for s in range(2):
            quantize(0, s)
        cast(2)
        gather(2, 0)
        cast(3)
        w_codes = keep.tile([P, PASSES, N], U32, name="w_codes", tag="raw3_0", align_bytes=64)
        nc.sync.dma_start(
            out=w_codes[:].bitcast(I32),
            in_=w1_words.rearrange("g p n t -> p g (n t)").bitcast(I32),
        )
        for j in range(BLOCKS):
            multiply(0, j)
        for s in range(SLICES):
            gather(3, s)
            weave(1, s, True)
        for s in range(SLICES):
            quantize(1, s)
            multiply(1, 2 * s)
            multiply(1, 2 * s + 1)
        for s in range(SLICES - 1):
            correct(2 * s)
            correct(2 * s + 1)
            finish((2 * s, 2 * s + 1), 2 * s, s == SLICES - 2)
        for i in range(2):
            correct(BLOCKS - 2 + i)
            finish((BLOCKS - 2 + i,), 2 * i, True)
